import numpy as np
import ml_dtypes


def mxq(x, axis, fmt="e4m3"):
    dtype, down = {"e4m3": (ml_dtypes.float8_e4m3fn, 7), "e5m2": (ml_dtypes.float8_e5m2, 14)}[fmt]
    v = np.moveaxis(np.asarray(x, np.float32).astype(ml_dtypes.bfloat16).astype(np.float64), axis, -1)
    blocks = v.reshape(v.shape[:-1] + (-1, 32))
    amax = np.abs(blocks).max(-1, keepdims=True)
    byte = np.maximum(np.where(amax > 0, np.frexp(amax)[1] - 1 + 127, 0) - down, 1)
    scale = np.exp2(byte - 127.0)
    codes = (blocks / scale).astype(np.float32).astype(dtype).astype(np.float64)
    return np.moveaxis((codes * scale).reshape(v.shape), -1, axis)


WIDE = False


def mx_kscale(k):
    if not WIDE:
        return np.ones(k)
    levels = np.array([30, -30])
    if k % 512:
        return np.exp2(np.random.permutation(np.resize(levels, k // 32))).repeat(32)
    a = np.empty((k // 512, 16))
    for p in range(k // 512):
        a[p, :8] = np.random.permutation(np.resize(levels, 8))
        for g in range(8):
            far = levels[np.abs(levels - a[p, g]) >= 10]
            a[p, g + 8] = far[np.random.randint(len(far))]
    return np.exp2(a.ravel()).repeat(32)


def f64(x):
    return np.asarray(x).astype(np.float64)


def striped(idx):
    return np.tile(np.asarray(idx).reshape(-1, 16).T, (8, 1)).astype(np.uint16)


def unstriped(offs):
    return offs[:16].T.reshape(-1).astype(np.int64)


E2M1 = np.array([0.0, 0.5, 1.0, 1.5, 2.0, 3.0, 4.0, 6.0, -0.0, -0.5, -1.0, -1.5, -2.0, -3.0, -4.0, -6.0])


def pack_weight(w, fmt):
    k, n = w.shape
    w = f64(np.asarray(w, np.float32).astype(ml_dtypes.bfloat16)).reshape(k // 32, 32, n)
    amax = np.abs(w).max(1)
    if fmt in ("e4m3", "e5m2"):
        byte = np.frexp(amax)[1] - 1 + 127 - (7 if fmt == "e4m3" else 14)
    else:
        mant, ex = np.frexp(amax / 6.0)
        byte = np.where(mant > 0.5, ex, ex - 1) + 127
    byte = np.clip(np.where(amax > 0, byte, 1), 1, 254)
    scaled = (w * np.exp2(127.0 - byte)[:, None, :]).reshape(k, n).astype(np.float32)
    by_word = np.ascontiguousarray(scaled.reshape(k // 512, 128, 4, n).transpose(0, 1, 3, 2))
    if fmt in ("e4m3", "e5m2"):
        words = by_word.astype(ml_dtypes.float8_e4m3fn if fmt == "e4m3" else ml_dtypes.float8_e5m2).view(np.uint8)
    else:
        c = by_word.astype(ml_dtypes.float4_e2m1fn).view(np.uint8) & 0xF
        words = (c[..., 0::2] | (c[..., 1::2] << 4)).reshape(k // 512, 128, 2 * n)
    return np.ascontiguousarray(words), np.ascontiguousarray(byte.astype(np.uint8).reshape(k // 512, 16, n))


def unpack_weight(words, scales, fmt):
    g, _, n = scales.shape
    words = np.ascontiguousarray(words).reshape(g, 128, n, -1)
    if fmt in ("e4m3", "e5m2"):
        vals = words.view(ml_dtypes.float8_e4m3fn if fmt == "e4m3" else ml_dtypes.float8_e5m2).astype(np.float64)
    else:
        nib = np.empty((g, 128, n, 4), np.uint8)
        nib[..., 0::2] = words & 0xF
        nib[..., 1::2] = words >> 4
        vals = E2M1[nib]
    vals = vals * np.repeat(np.exp2(scales.astype(np.float64) - 127.0), 8, axis=1)[..., None]
    return vals.transpose(0, 1, 3, 2).reshape(g * 512, n)


def e4m3fn_bytes(y):
    return np.clip(np.asarray(y, np.float64), -448.0, 448.0).astype(np.float32).astype(ml_dtypes.float8_e4m3fn).view(np.uint8)


def e4m3fn_values(b):
    return np.asarray(b, np.uint8).view(ml_dtypes.float8_e4m3fn).astype(np.float64)


K, T, J, R, F, Z, V, N = 512, 1024, 256, 512, 512, 1024, 1024, 256


def setup_inputs():
    n = np.random.standard_normal
    idx = np.random.permutation(T)[:J]
    idx2 = np.random.permutation(Z)[:J]
    idx3 = np.random.permutation(V)[:J]
    idx4 = np.random.permutation(V)[:J]
    fk = mx_kscale(K)
    ff = mx_kscale(F)
    fr = mx_kscale(R)
    xtp = pack_weight(n((K, T)) / fk[:, None], "e4m3")
    xop = pack_weight(n((F, Z)) / ff[:, None], "e2m1")
    wp = pack_weight(n((K, R)) * 1 / np.sqrt(K) * fk[:, None], "e2m1")
    w0p = pack_weight(n((F, R)) * 1 / np.sqrt(F) * ff[:, None], "e5m2")
    wbp = pack_weight(n((R, N)) * 1 / np.sqrt(R) / fr[:, None], "e5m2")
    return {
        "xt_words": xtp[0],
        "xt_scales": xtp[1],
        "xo_words": xop[0],
        "xo_scales": xop[1],
        "w_words": wp[0],
        "w_scales": wp[1],
        "w0_words": w0p[0],
        "w0_scales": w0p[1],
        "ca": e4m3fn_bytes(60.0 * n((R, V))),
        "st": (np.random.uniform(0.004, 0.012, (R, 1)) * fr[:, None]).astype(np.float32),
        "wb_words": wbp[0],
        "wb_scales": wbp[1],
        "offs": striped(idx),
        "offs2": striped(idx2),
        "offs3": striped(idx3),
        "offs4": striped(idx4),
    }


def reference(xt_words, xt_scales, xo_words, xo_scales, w_words, w_scales, w0_words, w0_scales, ca, st, wb_words, wb_scales, offs, offs2, offs3, offs4):
    idx = unstriped(offs)
    idx2 = unstriped(offs2)
    idx3 = unstriped(offs3)
    idx4 = unstriped(offs4)
    xtu = unpack_weight(xt_words, xt_scales, "e4m3")
    xou = unpack_weight(xo_words, xo_scales, "e2m1")
    wu = unpack_weight(w_words, w_scales, "e2m1")
    w0u = unpack_weight(w0_words, w0_scales, "e5m2")
    wbu = unpack_weight(wb_words, wb_scales, "e5m2")
    xtidxg = xtu[:, idx]
    xoidx2g = xou[:, idx2]
    a = wu.T @ xtidxg + w0u.T @ xoidx2g
    g1 = (e4m3fn_values(ca)[:, idx3] - e4m3fn_values(ca)[:, idx4]) * f64(st)
    hid = a * g1
    hidq = mxq(hid, 0, "e4m3")
    p = wbu.T @ hidq
    return p

@@ -1,0 +1,161 @@
+from contextlib import ExitStack
+
+import concourse.mybir as mybir
+from concourse.masks import make_identity
+
+F32 = mybir.dt.float32
+BF16 = mybir.dt.bfloat16
+I32 = mybir.dt.int32
+U32 = mybir.dt.uint32
+U16 = mybir.dt.uint16
+U8 = mybir.dt.uint8
+FP8 = mybir.dt.float8_e4m3fn
+E4M3X4 = mybir.dt.float8_e4m3fn_x4
+E5M2X4 = mybir.dt.float8_e5m2_x4
+E2M1X4 = mybir.dt.float4_e2m1fn_x4
+ALU = mybir.AluOpType
+ACT = mybir.ActivationFunctionType
+
+P = 128
+PACK = 4
+T, J, R, V, N = 1024, 256, 512, 1024, 256
+HALVES = J // P
+FLOPS = 2 * J * R * (512 + 512 + N)
+
+
+def tile_list_entrydiff_kernel(tc, xt_words, xt_scales, xo_words, xo_scales, w_words, w_scales, w0_words, w0_scales, ca, st, wb_words, wb_scales, offs, offs2, offs3, offs4, out):
+    nc = tc.nc
+    with ExitStack() as ctx:
+        lists = ctx.enter_context(tc.tile_pool(name="lists", bufs=1))
+        sb = ctx.enter_context(tc.tile_pool(name="sb", bufs=1))
+        ps = ctx.enter_context(tc.psum_pool(name="ps", bufs=1))
+
+        def tile(name, shape, dtype):
+            return sb.tile(shape, dtype, name=name, align_bytes=64)
+
+        def load_list(name, src):
+            t = lists.tile([P, J // 16], U16, name=name)
+            nc.sync.dma_start(t[:], src)
+            return t
+
+        def zeroed_plane(name, cols, engine):
+            plane = tile(name, [P, cols], U8)
+            engine.memset(plane[:].bitcast(I32), 0)
+            return plane
+
+        def load_scales(plane, src):
+            for q in range(4):
+                nc.sync.dma_start(plane[32 * q : 32 * q + 4, :].bitcast(I32), src[0, 4 * q : 4 * q + 4, :].bitcast(I32))
+
+        def load_words(name, src, cols, dtype):
+            t = tile(name, [P, cols], dtype)
+            nc.sync.dma_start(t[:].bitcast(I32), src.bitcast(I32))
+            return t
+
+        ca_rows = ca.rearrange("(p t) v -> p t v", t=PACK)
+
+        def load_ca(t):
+            tab = tile("ca%d" % t, [P, V], U8)
+            nc.sync.dma_start(tab[:], ca_rows[:, t, :])
+            return tab
+
+        xo_plane = zeroed_plane("xo_plane", T, nc.vector)
+        xt_plane = zeroed_plane("xt_plane", T, nc.vector)
+        st_sb = tile("st_sb", [P, PACK], F32)
+        nc.gpsimd.dma_start(st_sb[:], st.rearrange("(p t) o -> p (t o)", t=PACK))
+        w0_plane = zeroed_plane("w0_plane", R, nc.vector)
+        w_plane = zeroed_plane("w_plane", R, nc.vector)
+        wb_plane = zeroed_plane("wb_plane", N, nc.vector)
+        ident = tile("ident", [P, P], F32)
+        make_identity(nc, ident[:])
+
+        ca_sb = [None] * PACK
+        ca_sb[0] = load_ca(0)
+        l3 = load_list("l3", offs3)
+        l4 = load_list("l4", offs4)
+        ca_sb[1] = load_ca(1)
+        xo_sb = load_words("xo_sb", xo_words[0], T, U16)
+        l2 = load_list("l2", offs2)
+        l1 = load_list("l1", offs)
+        xt_sb = load_words("xt_sb", xt_words[0].rearrange("p c b -> p (c b)"), T, I32)
+        load_scales(xo_plane, xo_scales)
+        load_scales(xt_plane, xt_scales)
+        ca_sb[2] = load_ca(2)
+        w0_sb = load_words("w0_sb", w0_words[0].rearrange("p c b -> p (c b)"), R, I32)
+        w_sb = load_words("w_sb", w_words[0], 2 * R, U8)
+        load_scales(w0_plane, w0_scales)
+        load_scales(w_plane, w_scales)
+        ca_sb[3] = load_ca(3)
+        wb_sb = load_words("wb_sb", wb_words[0].rearrange("p c b -> p (c b)"), N, I32)
+        load_scales(wb_plane, wb_scales)
+
+        s3 = tile("s3", [P, PACK, J], F32)
+        s4 = tile("s4", [P, PACK, J], F32)
+
+        def look_up(t):
+            for name, lst, scaled in (("g3", l3, s3), ("g4", l4, s4)):
+                got = tile("%s_%d" % (name, t), [P, J], U8)
+                nc.vector.tensor_copy(got[:], ca_sb[t][:].indirect(lst[:]))
+                nc.scalar.activation(scaled[:, t, :], got[:].bitcast(FP8), ACT.Copy, scale=st_sb[:, t : t + 1])
+
+        look_up(0)
+        look_up(1)
+        xo_g = tile("xo_g", [P, J], U16)
+        nc.vector.tensor_copy(xo_g[:], xo_sb[:].indirect(l2[:]))
+        xt_g = tile("xt_g", [P, J], U32)
+        nc.vector.tensor_copy(xt_g[:], xt_sb[:].bitcast(U32).indirect(l1[:]))
+        xo_gs = tile("xo_gs", [P, J], U8)
+        nc.vector.tensor_copy(xo_gs[:], xo_plane[:].indirect(l2[:]))
+        xt_gs = tile("xt_gs", [P, J], U8)
+        nc.vector.tensor_copy(xt_gs[:], xt_plane[:].indirect(l1[:]))
+
+        at_ps = [ps.tile([P, R], F32, name="at_ps%d" % h) for h in range(HALVES)]
+        a_ps = [ps.tile([P, PACK, P], F32, name="a_ps%d" % h) for h in range(HALVES)]
+        for h in range(HALVES):
+            cols = slice(h * P, (h + 1) * P)
+            nc.tensor.matmul_mx(at_ps[h][:], lhsT=xo_g[:, cols].bitcast(E2M1X4), lhsT_scale=xo_gs[:, cols],
+                                rhs=w0_sb[:].bitcast(E5M2X4), rhs_scale=w0_plane[:], start=True, stop=False)
+        for h in range(HALVES):
+            cols = slice(h * P, (h + 1) * P)
+            nc.tensor.matmul_mx(at_ps[h][:], lhsT=xt_g[:, cols].bitcast(E4M3X4), lhsT_scale=xt_gs[:, cols],
+                                rhs=w_sb[:].bitcast(E2M1X4), rhs_scale=w_plane[:], start=False, stop=True)
+        for h in range(HALVES):
+            at_sb = tile("at_sb%d" % h, [P, PACK, P], F32)
+            nc.scalar.copy(at_sb[:], at_ps[h][:].rearrange("j (p t) -> j t p", t=PACK))
+            for t in range(PACK):
+                nc.tensor.transpose(a_ps[h][:, t, :], at_sb[:, t, :], ident[:])
+
+        look_up(2)
+        look_up(3)
+
+        d = tile("d", [P, PACK, J], F32)
+        for t in range(PACK):
+            nc.vector.tensor_tensor(d[:, t, :], s3[:, t, :], s4[:, t, :], ALU.subtract)
+
+        hid = [tile("hid%d" % h, [P, P * PACK], BF16) for h in range(HALVES)]
+        for h in range(HALVES):
+            nc.vector.tensor_tensor(
+                hid[h][:].rearrange("p (c i t) -> p c t i", i=4, t=PACK),
+                a_ps[h][:].rearrange("p t (c i) -> p c t i", i=4),
+                d[:, :, h * P : (h + 1) * P].rearrange("p t (c i) -> p c t i", i=4),
+                ALU.mult,
+            )
+        hq = [tile("hq%d" % h, [P, P], U32) for h in range(HALVES)]
+        hq_plane = [tile("hq_plane%d" % h, [P, P], U8) for h in range(HALVES)]
+        for h in range(HALVES):
+            nc.vector.quantize_mx(hq[h][:].bitcast(E4M3X4), hq_plane[h][:], hid[h][:])
+
+        out_rows = out.rearrange("(m p) j -> p m j", p=P)
+        for h in range(HALVES):
+            o_ps = ps.tile([P, N // P, P], F32, name="o_ps%d" % h)
+            for m in range(N // P):
+                rows = slice(m * P, (m + 1) * P)
+                nc.tensor.matmul_mx(o_ps[:, m, :], lhsT=wb_sb[:, rows].bitcast(E5M2X4), lhsT_scale=wb_plane[:, rows],
+                                    rhs=hq[h][:].bitcast(E4M3X4), rhs_scale=hq_plane[h][:], start=True, stop=True)
+            o_sb = tile("o_sb%d" % h, [P, N // P, P], F32)
+            if h == 0:
+                nc.scalar.copy(o_sb[:], o_ps[:])
+                nc.scalar.dma_start(out_rows[:, :, h * P : (h + 1) * P], o_sb[:])
+            else:
+                nc.vector.tensor_copy(o_sb[:], o_ps[:])
+                nc.sync.dma_start(out_rows[:, :, h * P : (h + 1) * P], o_sb[:])

@@ -1,7 +1,6 @@
 from contextlib import ExitStack
 
 import concourse.mybir as mybir
-from concourse.masks import make_identity
 
 F32 = mybir.dt.float32
 BF16 = mybir.dt.bfloat16
@@ -30,8 +29,8 @@ def tile_list_entrydiff_kernel(tc, xt_words, xt_scales, xo_words, xo_scales, w_w
         sb = ctx.enter_context(tc.tile_pool(name="sb", bufs=1))
         ps = ctx.enter_context(tc.psum_pool(name="ps", bufs=1))
 
-        def tile(name, shape, dtype):
-            return sb.tile(shape, dtype, name=name, align_bytes=64)
+        def tile(name, shape, dtype, tag=None):
+            return sb.tile(shape, dtype, name=name, tag=tag or name, align_bytes=64)
 
         def load_list(name, src):
             t = lists.tile([P, J // 16], U16, name=name)
@@ -43,9 +42,24 @@ def tile_list_entrydiff_kernel(tc, xt_words, xt_scales, xo_words, xo_scales, w_w
             engine.memset(plane[:].bitcast(I32), 0)
             return plane
 
-        def load_scales(plane, src):
+        def load_scales(plane, src, queue):
             for q in range(4):
-                nc.sync.dma_start(plane[32 * q : 32 * q + 4, :].bitcast(I32), src[0, 4 * q : 4 * q + 4, :].bitcast(I32))
+                queue.dma_start(plane[32 * q : 32 * q + 4, :].bitcast(I32), src[0, 4 * q : 4 * q + 4, :].bitcast(I32))
+
+        def paired_plane(name, cols):
+            plane = tile(name, [P, 2 * cols], U8)
+            nc.vector.memset(plane[0:64, :].bitcast(I32), 0)
+            return plane
+
+        def load_scale_pairs(plane, src, queue):
+            rows = src[0].rearrange("(u q r) c -> q r u c", u=2, q=2).bitcast(I32)
+            for q in range(2):
+                queue.dma_start(plane[32 * q : 32 * q + 4, :].bitcast(I32).rearrange("r (u c) -> r u c", u=2), rows[q])
+
+        def spread(plane):
+            cols = plane.shape[1] // 2
+            nc.vector.tensor_copy(plane[64:128, 0:cols].bitcast(I32), plane[0:64, cols : 2 * cols].bitcast(I32))
+            return plane[:, 0:cols]
 
         def load_words(name, src, cols, dtype):
             t = tile(name, [P, cols], dtype)
@@ -59,78 +73,75 @@ def tile_list_entrydiff_kernel(tc, xt_words, xt_scales, xo_words, xo_scales, w_w
             nc.sync.dma_start(tab[:], ca_rows[:, t, :])
             return tab
 
-        xo_plane = zeroed_plane("xo_plane", T, nc.vector)
-        xt_plane = zeroed_plane("xt_plane", T, nc.vector)
         st_sb = tile("st_sb", [P, PACK], F32)
         nc.gpsimd.dma_start(st_sb[:], st.rearrange("(p t) o -> p (t o)", t=PACK))
-        w0_plane = zeroed_plane("w0_plane", R, nc.vector)
-        w_plane = zeroed_plane("w_plane", R, nc.vector)
-        wb_plane = zeroed_plane("wb_plane", N, nc.vector)
-        ident = tile("ident", [P, P], F32)
-        make_identity(nc, ident[:])
+        xo_plane = zeroed_plane("xo_plane", T, nc.vector)
+        w0_pairs = paired_plane("w0_pairs", R)
+        xt_plane = zeroed_plane("xt_plane", T, nc.vector)
+        w_pairs = paired_plane("w_pairs", R)
+        wb_pairs = paired_plane("wb_pairs", N)
 
         ca_sb = [None] * PACK
         ca_sb[0] = load_ca(0)
         l3 = load_list("l3", offs3)
         l4 = load_list("l4", offs4)
         ca_sb[1] = load_ca(1)
-        xo_sb = load_words("xo_sb", xo_words[0], T, U16)
         l2 = load_list("l2", offs2)
         l1 = load_list("l1", offs)
-        xt_sb = load_words("xt_sb", xt_words[0].rearrange("p c b -> p (c b)"), T, I32)
-        load_scales(xo_plane, xo_scales)
-        load_scales(xt_plane, xt_scales)
         ca_sb[2] = load_ca(2)
-        w0_sb = load_words("w0_sb", w0_words[0].rearrange("p c b -> p (c b)"), R, I32)
-        w_sb = load_words("w_sb", w_words[0], 2 * R, U8)
-        load_scales(w0_plane, w0_scales)
-        load_scales(w_plane, w_scales)
+        xo_sb = load_words("xo_sb", xo_words[0], T, U16)
         ca_sb[3] = load_ca(3)
+        load_scales(xo_plane, xo_scales, nc.sync)
+        load_scale_pairs(w0_pairs, w0_scales, nc.sync)
+        xt_sb = load_words("xt_sb", xt_words[0].rearrange("p c b -> p (c b)"), T, I32)
+        w0_sb = load_words("w0_sb", w0_words[0].rearrange("p c b -> p (c b)"), R, U32)
+        w_sb = load_words("w_sb", w_words[0], R, U16)
+        load_scale_pairs(w_pairs, w_scales, nc.sync)
+        load_scales(xt_plane, xt_scales, nc.sync)
         wb_sb = load_words("wb_sb", wb_words[0].rearrange("p c b -> p (c b)"), N, I32)
-        load_scales(wb_plane, wb_scales)
+        load_scale_pairs(wb_pairs, wb_scales, nc.sync)
 
         s3 = tile("s3", [P, PACK, J], F32)
         s4 = tile("s4", [P, PACK, J], F32)
-
-        def look_up(t):
+        for t in range(PACK):
             for name, lst, scaled in (("g3", l3, s3), ("g4", l4, s4)):
                 got = tile("%s_%d" % (name, t), [P, J], U8)
                 nc.vector.tensor_copy(got[:], ca_sb[t][:].indirect(lst[:]))
                 nc.scalar.activation(scaled[:, t, :], got[:].bitcast(FP8), ACT.Copy, scale=st_sb[:, t : t + 1])
 
-        look_up(0)
-        look_up(1)
+        def dealt(name, words, pairs, dtype):
+            dealt_words = tile(name + "_words", [P, PACK, P], dtype)
+            nc.scalar.copy(dealt_words[:], words[:].rearrange("k (m t) -> k t m", t=PACK))
+            dealt_plane = tile(name + "_plane", [P, PACK, P], U8)
+            nc.vector.tensor_copy(dealt_plane[:], spread(pairs).rearrange("k (m t) -> k t m", t=PACK))
+            return dealt_words, dealt_plane
+
+        w0_d, w0_plane = dealt("w0_d", w0_sb, w0_pairs, U32)
+        w_d, w_plane = dealt("w_d", w_sb, w_pairs, U16)
+
+        a_ps = [ps.tile([P, PACK, P], F32, name="a_ps%d" % h) for h in range(HALVES)]
         xo_g = tile("xo_g", [P, J], U16)
         nc.vector.tensor_copy(xo_g[:], xo_sb[:].indirect(l2[:]))
-        xt_g = tile("xt_g", [P, J], U32)
-        nc.vector.tensor_copy(xt_g[:], xt_sb[:].bitcast(U32).indirect(l1[:]))
         xo_gs = tile("xo_gs", [P, J], U8)
         nc.vector.tensor_copy(xo_gs[:], xo_plane[:].indirect(l2[:]))
+        for h in range(HALVES):
+            cols = slice(h * P, (h + 1) * P)
+            for t in range(PACK):
+                nc.tensor.matmul_mx(a_ps[h][:, t, :], lhsT=w0_d[:, t, :].bitcast(E5M2X4), lhsT_scale=w0_plane[:, t, :],
+                                    rhs=xo_g[:, cols].bitcast(E2M1X4), rhs_scale=xo_gs[:, cols], start=t == 0, stop=False)
+        xt_g = tile("xt_g", [P, J], U32)
+        nc.vector.tensor_copy(xt_g[:], xt_sb[:].bitcast(U32).indirect(l1[:]))
         xt_gs = tile("xt_gs", [P, J], U8)
         nc.vector.tensor_copy(xt_gs[:], xt_plane[:].indirect(l1[:]))
-
-        at_ps = [ps.tile([P, R], F32, name="at_ps%d" % h) for h in range(HALVES)]
-        a_ps = [ps.tile([P, PACK, P], F32, name="a_ps%d" % h) for h in range(HALVES)]
         for h in range(HALVES):
             cols = slice(h * P, (h + 1) * P)
-            nc.tensor.matmul_mx(at_ps[h][:], lhsT=xo_g[:, cols].bitcast(E2M1X4), lhsT_scale=xo_gs[:, cols],
-                                rhs=w0_sb[:].bitcast(E5M2X4), rhs_scale=w0_plane[:], start=True, stop=False)
-        for h in range(HALVES):
-            cols = slice(h * P, (h + 1) * P)
-            nc.tensor.matmul_mx(at_ps[h][:], lhsT=xt_g[:, cols].bitcast(E4M3X4), lhsT_scale=xt_gs[:, cols],
-                                rhs=w_sb[:].bitcast(E2M1X4), rhs_scale=w_plane[:], start=False, stop=True)
-        for h in range(HALVES):
-            at_sb = tile("at_sb%d" % h, [P, PACK, P], F32)
-            nc.scalar.copy(at_sb[:], at_ps[h][:].rearrange("j (p t) -> j t p", t=PACK))
             for t in range(PACK):
-                nc.tensor.transpose(a_ps[h][:, t, :], at_sb[:, t, :], ident[:])
+                nc.tensor.matmul_mx(a_ps[h][:, t, :], lhsT=w_d[:, t, :].bitcast(E2M1X4), lhsT_scale=w_plane[:, t, :],
+                                    rhs=xt_g[:, cols].bitcast(E4M3X4), rhs_scale=xt_gs[:, cols], start=False, stop=t == PACK - 1)
 
-        look_up(2)
-        look_up(3)
-
-        d = tile("d", [P, PACK, J], F32)
-        for t in range(PACK):
-            nc.vector.tensor_tensor(d[:, t, :], s3[:, t, :], s4[:, t, :], ALU.subtract)
+        d = tile("d", [P, PACK, J], F32, tag="xt_plane")
+        nc.vector.tensor_tensor(d[:], s3[:], s4[:], ALU.subtract)
+        wb_plane = spread(wb_pairs)
 
         hid = [tile("hid%d" % h, [P, P * PACK], BF16) for h in range(HALVES)]
         for h in range(HALVES):

@@ -42,8 +42,8 @@ def tile_list_entrydiff_kernel(tc, xt_words, xt_scales, xo_words, xo_scales, w_w
             engine.memset(plane[:].bitcast(I32), 0)
             return plane
 
-        def load_scales(plane, src, queue):
-            for q in range(4):
+        def load_scales(plane, src, queue, quadrants):
+            for q in quadrants:
                 queue.dma_start(plane[32 * q : 32 * q + 4, :].bitcast(I32), src[0, 4 * q : 4 * q + 4, :].bitcast(I32))
 
         def paired_plane(name, cols):
@@ -75,11 +75,11 @@ def tile_list_entrydiff_kernel(tc, xt_words, xt_scales, xo_words, xo_scales, w_w
 
         st_sb = tile("st_sb", [P, PACK], F32)
         nc.gpsimd.dma_start(st_sb[:], st.rearrange("(p t) o -> p (t o)", t=PACK))
-        xo_plane = zeroed_plane("xo_plane", T, nc.vector)
         w0_pairs = paired_plane("w0_pairs", R)
-        xt_plane = zeroed_plane("xt_plane", T, nc.vector)
+        xo_plane = zeroed_plane("xo_plane", T, nc.vector)
         w_pairs = paired_plane("w_pairs", R)
-        wb_pairs = paired_plane("wb_pairs", N)
+        xt_plane = zeroed_plane("xt_plane", T, nc.vector)
+        wb_plane = zeroed_plane("wb_plane", N, nc.vector)
 
         ca_sb = [None] * PACK
         ca_sb[0] = load_ca(0)
@@ -90,16 +90,16 @@ def tile_list_entrydiff_kernel(tc, xt_words, xt_scales, xo_words, xo_scales, w_w
         l1 = load_list("l1", offs)
         ca_sb[2] = load_ca(2)
         xo_sb = load_words("xo_sb", xo_words[0], T, U16)
-        ca_sb[3] = load_ca(3)
-        load_scales(xo_plane, xo_scales, nc.sync)
         load_scale_pairs(w0_pairs, w0_scales, nc.sync)
+        ca_sb[3] = load_ca(3)
+        load_scales(xo_plane, xo_scales, nc.sync, range(4))
+        load_scale_pairs(w_pairs, w_scales, nc.sync)
         xt_sb = load_words("xt_sb", xt_words[0].rearrange("p c b -> p (c b)"), T, I32)
         w0_sb = load_words("w0_sb", w0_words[0].rearrange("p c b -> p (c b)"), R, U32)
         w_sb = load_words("w_sb", w_words[0], R, U16)
-        load_scale_pairs(w_pairs, w_scales, nc.sync)
-        load_scales(xt_plane, xt_scales, nc.sync)
+        load_scales(xt_plane, xt_scales, nc.sync, range(4))
         wb_sb = load_words("wb_sb", wb_words[0].rearrange("p c b -> p (c b)"), N, I32)
-        load_scale_pairs(wb_pairs, wb_scales, nc.sync)
+        load_scales(wb_plane, wb_scales, nc.sync, range(4))
 
         s3 = tile("s3", [P, PACK, J], F32)
         s4 = tile("s4", [P, PACK, J], F32)
@@ -111,9 +111,9 @@ def tile_list_entrydiff_kernel(tc, xt_words, xt_scales, xo_words, xo_scales, w_w
 
         def dealt(name, words, pairs, dtype):
             dealt_words = tile(name + "_words", [P, PACK, P], dtype)
-            nc.scalar.copy(dealt_words[:], words[:].rearrange("k (m t) -> k t m", t=PACK))
+            nc.scalar.copy(dealt_words[:].rearrange("k t (c i) -> k c t i", i=4), words[:].rearrange("k (c i t) -> k c t i", i=4, t=PACK))
             dealt_plane = tile(name + "_plane", [P, PACK, P], U8)
-            nc.vector.tensor_copy(dealt_plane[:], spread(pairs).rearrange("k (m t) -> k t m", t=PACK))
+            nc.gpsimd.tensor_copy(dealt_plane[:], spread(pairs).rearrange("k (m t) -> k t m", t=PACK))
             return dealt_words, dealt_plane
 
         w0_d, w0_plane = dealt("w0_d", w0_sb, w0_pairs, U32)
@@ -141,14 +141,13 @@ def tile_list_entrydiff_kernel(tc, xt_words, xt_scales, xo_words, xo_scales, w_w
 
         d = tile("d", [P, PACK, J], F32, tag="xt_plane")
         nc.vector.tensor_tensor(d[:], s3[:], s4[:], ALU.subtract)
-        wb_plane = spread(wb_pairs)
 
         hid = [tile("hid%d" % h, [P, P * PACK], BF16) for h in range(HALVES)]
         for h in range(HALVES):
             nc.vector.tensor_tensor(
-                hid[h][:].rearrange("p (c i t) -> p c t i", i=4, t=PACK),
-                a_ps[h][:].rearrange("p t (c i) -> p c t i", i=4),
-                d[:, :, h * P : (h + 1) * P].rearrange("p t (c i) -> p c t i", i=4),
+                hid[h][:].rearrange("p (c i t) -> p c t i", i=2, t=PACK),
+                a_ps[h][:].rearrange("p t (c i) -> p c t i", i=2),
+                d[:, :, h * P : (h + 1) * P].rearrange("p t (c i) -> p c t i", i=2),
                 ALU.mult,
             )
         hq = [tile("hq%d" % h, [P, P], U32) for h in range(HALVES)]
@@ -156,17 +155,17 @@ def tile_list_entrydiff_kernel(tc, xt_words, xt_scales, xo_words, xo_scales, w_w
         for h in range(HALVES):
             nc.vector.quantize_mx(hq[h][:].bitcast(E4M3X4), hq_plane[h][:], hid[h][:])
 
-        out_rows = out.rearrange("(m p) j -> p m j", p=P)
+        o_sb = [tile("o_sb%d" % m, [P, J], F32) for m in range(N // P)]
         for h in range(HALVES):
-            o_ps = ps.tile([P, N // P, P], F32, name="o_ps%d" % h)
+            cols = slice(h * P, (h + 1) * P)
             for m in range(N // P):
                 rows = slice(m * P, (m + 1) * P)
-                nc.tensor.matmul_mx(o_ps[:, m, :], lhsT=wb_sb[:, rows].bitcast(E5M2X4), lhsT_scale=wb_plane[:, rows],
+                o_ps = ps.tile([P, P], F32, name="o_ps%d_%d" % (h, m))
+                nc.tensor.matmul_mx(o_ps[:], lhsT=wb_sb[:, rows].bitcast(E5M2X4), lhsT_scale=wb_plane[:, rows],
                                     rhs=hq[h][:].bitcast(E4M3X4), rhs_scale=hq_plane[h][:], start=True, stop=True)
-            o_sb = tile("o_sb%d" % h, [P, N // P, P], F32)
-            if h == 0:
-                nc.scalar.copy(o_sb[:], o_ps[:])
-                nc.scalar.dma_start(out_rows[:, :, h * P : (h + 1) * P], o_sb[:])
-            else:
-                nc.vector.tensor_copy(o_sb[:], o_ps[:])
-                nc.sync.dma_start(out_rows[:, :, h * P : (h + 1) * P], o_sb[:])
+                if m == 0:
+                    nc.scalar.copy(o_sb[m][:, cols], o_ps[:])
+                else:
+                    nc.vector.tensor_copy(o_sb[m][:, cols], o_ps[:])
+        nc.scalar.dma_start(out[0:P, :], o_sb[0][:])
+        nc.sync.dma_start(out[P : 2 * P, :], o_sb[1][:])

@@ -1,6 +1,7 @@
 from contextlib import ExitStack
 
 import concourse.mybir as mybir
+from concourse.masks import make_identity
 
 F32 = mybir.dt.float32
 BF16 = mybir.dt.bfloat16
@@ -19,6 +20,7 @@ P = 128
 PACK = 4
 T, J, R, V, N = 1024, 256, 512, 1024, 256
 HALVES = J // P
+EARLY = 2
 FLOPS = 2 * J * R * (512 + 512 + N)
 
 
@@ -46,21 +48,6 @@ def tile_list_entrydiff_kernel(tc, xt_words, xt_scales, xo_words, xo_scales, w_w
             for q in quadrants:
                 queue.dma_start(plane[32 * q : 32 * q + 4, :].bitcast(I32), src[0, 4 * q : 4 * q + 4, :].bitcast(I32))
 
-        def paired_plane(name, cols):
-            plane = tile(name, [P, 2 * cols], U8)
-            nc.vector.memset(plane[0:64, :].bitcast(I32), 0)
-            return plane
-
-        def load_scale_pairs(plane, src, queue):
-            rows = src[0].rearrange("(u q r) c -> q r u c", u=2, q=2).bitcast(I32)
-            for q in range(2):
-                queue.dma_start(plane[32 * q : 32 * q + 4, :].bitcast(I32).rearrange("r (u c) -> r u c", u=2), rows[q])
-
-        def spread(plane):
-            cols = plane.shape[1] // 2
-            nc.vector.tensor_copy(plane[64:128, 0:cols].bitcast(I32), plane[0:64, cols : 2 * cols].bitcast(I32))
-            return plane[:, 0:cols]
-
         def load_words(name, src, cols, dtype):
             t = tile(name, [P, cols], dtype)
             nc.sync.dma_start(t[:].bitcast(I32), src.bitcast(I32))
@@ -75,9 +62,9 @@ def tile_list_entrydiff_kernel(tc, xt_words, xt_scales, xo_words, xo_scales, w_w
 
         st_sb = tile("st_sb", [P, PACK], F32)
         nc.gpsimd.dma_start(st_sb[:], st.rearrange("(p t) o -> p (t o)", t=PACK))
-        w0_pairs = paired_plane("w0_pairs", R)
+        w0_plane = zeroed_plane("w0_plane", R, nc.vector)
         xo_plane = zeroed_plane("xo_plane", T, nc.vector)
-        w_pairs = paired_plane("w_pairs", R)
+        w_plane = zeroed_plane("w_plane", R, nc.vector)
         xt_plane = zeroed_plane("xt_plane", T, nc.vector)
         wb_plane = zeroed_plane("wb_plane", N, nc.vector)
 
@@ -90,34 +77,57 @@ def tile_list_entrydiff_kernel(tc, xt_words, xt_scales, xo_words, xo_scales, w_w
         l1 = load_list("l1", offs)
         ca_sb[2] = load_ca(2)
         xo_sb = load_words("xo_sb", xo_words[0], T, U16)
-        load_scale_pairs(w0_pairs, w0_scales, nc.sync)
-        ca_sb[3] = load_ca(3)
-        load_scales(xo_plane, xo_scales, nc.sync, range(4))
-        load_scale_pairs(w_pairs, w_scales, nc.sync)
-        xt_sb = load_words("xt_sb", xt_words[0].rearrange("p c b -> p (c b)"), T, I32)
         w0_sb = load_words("w0_sb", w0_words[0].rearrange("p c b -> p (c b)"), R, U32)
+        load_scales(w0_plane, w0_scales, nc.sync, range(4))
+        load_scales(xo_plane, xo_scales, nc.sync, range(4))
+        ca_sb[3] = load_ca(3)
         w_sb = load_words("w_sb", w_words[0], R, U16)
+        load_scales(w_plane, w_scales, nc.sync, range(4))
+        xt_sb = load_words("xt_sb", xt_words[0].rearrange("p c b -> p (c b)"), T, I32)
         load_scales(xt_plane, xt_scales, nc.sync, range(4))
         wb_sb = load_words("wb_sb", wb_words[0].rearrange("p c b -> p (c b)"), N, I32)
         load_scales(wb_plane, wb_scales, nc.sync, range(4))
 
-        s3 = tile("s3", [P, PACK, J], F32)
-        s4 = tile("s4", [P, PACK, J], F32)
-        for t in range(PACK):
-            for name, lst, scaled in (("g3", l3, s3), ("g4", l4, s4)):
-                got = tile("%s_%d" % (name, t), [P, J], U8)
-                nc.vector.tensor_copy(got[:], ca_sb[t][:].indirect(lst[:]))
-                nc.scalar.activation(scaled[:, t, :], got[:].bitcast(FP8), ACT.Copy, scale=st_sb[:, t : t + 1])
+        ident = tile("ident", [P, P], F32)
+        make_identity(nc, ident[:])
 
-        def dealt(name, words, pairs, dtype):
+        def look_up(name, lst, t, values, scale):
+            got = tile("%s_%d" % (name, t), [P, J], U8)
+            nc.vector.tensor_copy(got[:], ca_sb[t][:].indirect(lst[:]))
+            nc.scalar.activation(values, got[:].bitcast(FP8), ACT.Copy, scale=scale)
+
+        turned_ps = ps.tile([P, EARLY, HALVES, P], F32, name="turned_ps")
+        for t in range(EARLY):
+            plus = tile("plus%d" % t, [P, J], F32)
+            minus = tile("minus%d" % t, [P, J], F32)
+            look_up("g3", l3, t, plus[:], 1.0)
+            look_up("g4", l4, t, minus[:], -1.0)
+            for h in range(HALVES):
+                cols = slice(h * P, (h + 1) * P)
+                nc.tensor.matmul(turned_ps[:, t, h, :], plus[:, cols], ident[:], start=True, stop=False, is_transpose=True)
+                nc.tensor.matmul(turned_ps[:, t, h, :], minus[:, cols], ident[:], start=False, stop=True, is_transpose=True)
+        turned = tile("turned", [P, EARLY, HALVES, P], F32)
+        nc.scalar.copy(turned[:], turned_ps[:])
+        early_ps = ps.tile([P, HALVES, EARLY, P], F32, name="early_ps")
+        for t in range(EARLY):
+            for h in range(HALVES):
+                nc.tensor.transpose(early_ps[:, h, t, :], turned[:, t, h, :], ident[:])
+
+        s3 = tile("s3", [P, PACK - EARLY, J], F32)
+        s4 = tile("s4", [P, PACK - EARLY, J], F32)
+        for t in range(EARLY, PACK):
+            look_up("g3", l3, t, s3[:, t - EARLY, :], st_sb[:, t : t + 1])
+            look_up("g4", l4, t, s4[:, t - EARLY, :], st_sb[:, t : t + 1])
+
+        def dealt(name, words, plane, dtype):
             dealt_words = tile(name + "_words", [P, PACK, P], dtype)
             nc.scalar.copy(dealt_words[:].rearrange("k t (c i) -> k c t i", i=4), words[:].rearrange("k (c i t) -> k c t i", i=4, t=PACK))
             dealt_plane = tile(name + "_plane", [P, PACK, P], U8)
-            nc.gpsimd.tensor_copy(dealt_plane[:], spread(pairs).rearrange("k (m t) -> k t m", t=PACK))
+            nc.gpsimd.tensor_copy(dealt_plane[:], plane[:].rearrange("k (m t) -> k t m", t=PACK))
             return dealt_words, dealt_plane
 
-        w0_d, w0_plane = dealt("w0_d", w0_sb, w0_pairs, U32)
-        w_d, w_plane = dealt("w_d", w_sb, w_pairs, U16)
+        w0_d, w0_ds = dealt("w0_d", w0_sb, w0_plane, U32)
+        w_d, w_ds = dealt("w_d", w_sb, w_plane, U16)
 
         a_ps = [ps.tile([P, PACK, P], F32, name="a_ps%d" % h) for h in range(HALVES)]
         xo_g = tile("xo_g", [P, J], U16)
@@ -127,27 +137,31 @@ def tile_list_entrydiff_kernel(tc, xt_words, xt_scales, xo_words, xo_scales, w_w
         for h in range(HALVES):
             cols = slice(h * P, (h + 1) * P)
             for t in range(PACK):
-                nc.tensor.matmul_mx(a_ps[h][:, t, :], lhsT=w0_d[:, t, :].bitcast(E5M2X4), lhsT_scale=w0_plane[:, t, :],
+                nc.tensor.matmul_mx(a_ps[h][:, t, :], lhsT=w0_d[:, t, :].bitcast(E5M2X4), lhsT_scale=w0_ds[:, t, :],
                                     rhs=xo_g[:, cols].bitcast(E2M1X4), rhs_scale=xo_gs[:, cols], start=t == 0, stop=False)
         xt_g = tile("xt_g", [P, J], U32)
         nc.vector.tensor_copy(xt_g[:], xt_sb[:].bitcast(U32).indirect(l1[:]))
-        xt_gs = tile("xt_gs", [P, J], U8)
-        nc.vector.tensor_copy(xt_gs[:], xt_plane[:].indirect(l1[:]))
         for h in range(HALVES):
             cols = slice(h * P, (h + 1) * P)
+            xt_gs = tile("xt_gs%d" % h, [P, P], U8)
+            nc.vector.tensor_copy(xt_gs[:], xt_plane[:].indirect(l1[:, h * P // 16 : (h + 1) * P // 16]))
             for t in range(PACK):
-                nc.tensor.matmul_mx(a_ps[h][:, t, :], lhsT=w_d[:, t, :].bitcast(E2M1X4), lhsT_scale=w_plane[:, t, :],
-                                    rhs=xt_g[:, cols].bitcast(E4M3X4), rhs_scale=xt_gs[:, cols], start=False, stop=t == PACK - 1)
+                nc.tensor.matmul_mx(a_ps[h][:, t, :], lhsT=w_d[:, t, :].bitcast(E2M1X4), lhsT_scale=w_ds[:, t, :],
+                                    rhs=xt_g[:, cols].bitcast(E4M3X4), rhs_scale=xt_gs[:], start=False, stop=t == PACK - 1)
 
-        d = tile("d", [P, PACK, J], F32, tag="xt_plane")
-        nc.vector.tensor_tensor(d[:], s3[:], s4[:], ALU.subtract)
+        d = tile("d", [P, HALVES, PACK, P], F32, tag="xt_plane")
+        for h in range(HALVES):
+            cols = slice(h * P, (h + 1) * P)
+            for t in range(EARLY):
+                nc.scalar.activation(d[:, h, t, :], early_ps[:, h, t, :], ACT.Copy, scale=st_sb[:, t : t + 1])
+            nc.vector.tensor_tensor(d[:, h, EARLY:PACK, :], s3[:, :, cols], s4[:, :, cols], ALU.subtract)
 
         hid = [tile("hid%d" % h, [P, P * PACK], BF16) for h in range(HALVES)]
         for h in range(HALVES):
             nc.vector.tensor_tensor(
                 hid[h][:].rearrange("p (c i t) -> p c t i", i=2, t=PACK),
                 a_ps[h][:].rearrange("p t (c i) -> p c t i", i=2),
-                d[:, :, h * P : (h + 1) * P].rearrange("p t (c i) -> p c t i", i=2),
+                d[:, h].rearrange("p t (c i) -> p c t i", i=2),
                 ALU.mult,
             )
         hq = [tile("hq%d" % h, [P, P], U32) for h in range(HALVES)]
@@ -155,7 +169,6 @@ def tile_list_entrydiff_kernel(tc, xt_words, xt_scales, xo_words, xo_scales, w_w
         for h in range(HALVES):
             nc.vector.quantize_mx(hq[h][:].bitcast(E4M3X4), hq_plane[h][:], hid[h][:])
 
-        o_sb = [tile("o_sb%d" % m, [P, J], F32) for m in range(N // P)]
         for h in range(HALVES):
             cols = slice(h * P, (h + 1) * P)
             for m in range(N // P):
@@ -163,9 +176,10 @@ def tile_list_entrydiff_kernel(tc, xt_words, xt_scales, xo_words, xo_scales, w_w
                 o_ps = ps.tile([P, P], F32, name="o_ps%d_%d" % (h, m))
                 nc.tensor.matmul_mx(o_ps[:], lhsT=wb_sb[:, rows].bitcast(E5M2X4), lhsT_scale=wb_plane[:, rows],
                                     rhs=hq[h][:].bitcast(E4M3X4), rhs_scale=hq_plane[h][:], start=True, stop=True)
+                o_sb = tile("o_sb%d_%d" % (h, m), [P, P], F32)
                 if m == 0:
-                    nc.scalar.copy(o_sb[m][:, cols], o_ps[:])
+                    nc.scalar.copy(o_sb[:], o_ps[:])
                 else:
-                    nc.vector.tensor_copy(o_sb[m][:, cols], o_ps[:])
-        nc.scalar.dma_start(out[0:P, :], o_sb[0][:])
-        nc.sync.dma_start(out[P : 2 * P, :], o_sb[1][:])
+                    nc.vector.tensor_copy(o_sb[:], o_ps[:])
+                queue = nc.scalar if (h, m) == (1, 0) else nc.sync
+                queue.dma_start(out[rows, cols], o_sb[:])

from contextlib import ExitStack

import concourse.mybir as mybir
from concourse.masks import make_identity

F32 = mybir.dt.float32
BF16 = mybir.dt.bfloat16
I32 = mybir.dt.int32
U32 = mybir.dt.uint32
U16 = mybir.dt.uint16
U8 = mybir.dt.uint8
FP8 = mybir.dt.float8_e4m3fn
E4M3X4 = mybir.dt.float8_e4m3fn_x4
E5M2X4 = mybir.dt.float8_e5m2_x4
E2M1X4 = mybir.dt.float4_e2m1fn_x4
ALU = mybir.AluOpType
ACT = mybir.ActivationFunctionType

P = 128
PACK = 4
T, J, R, V, N = 1024, 256, 512, 1024, 256
HALVES = J // P
EARLY = 2
FLOPS = 2 * J * R * (512 + 512 + N)


def tile_list_entrydiff_kernel(tc, xt_words, xt_scales, xo_words, xo_scales, w_words, w_scales, w0_words, w0_scales, ca, st, wb_words, wb_scales, offs, offs2, offs3, offs4, out):
    nc = tc.nc
    with ExitStack() as ctx:
        lists = ctx.enter_context(tc.tile_pool(name="lists", bufs=1))
        sb = ctx.enter_context(tc.tile_pool(name="sb", bufs=1))
        ps = ctx.enter_context(tc.psum_pool(name="ps", bufs=1))

        def tile(name, shape, dtype, tag=None):
            return sb.tile(shape, dtype, name=name, tag=tag or name, align_bytes=64)

        def load_list(name, src):
            t = lists.tile([P, J // 16], U16, name=name)
            nc.sync.dma_start(t[:], src)
            return t

        def zeroed_plane(name, cols, engine):
            plane = tile(name, [P, cols], U8)
            engine.memset(plane[:].bitcast(I32), 0)
            return plane

        def load_scales(plane, src, queue, quadrants):
            for q in quadrants:
                queue.dma_start(plane[32 * q : 32 * q + 4, :].bitcast(I32), src[0, 4 * q : 4 * q + 4, :].bitcast(I32))

        def load_words(name, src, cols, dtype):
            t = tile(name, [P, cols], dtype)
            nc.sync.dma_start(t[:].bitcast(I32), src.bitcast(I32))
            return t

        ca_rows = ca.rearrange("(p t) v -> p t v", t=PACK)

        def load_ca(t):
            tab = tile("ca%d" % t, [P, V], U8)
            nc.sync.dma_start(tab[:], ca_rows[:, t, :])
            return tab

        st_sb = tile("st_sb", [P, PACK], F32)
        nc.gpsimd.dma_start(st_sb[:], st.rearrange("(p t) o -> p (t o)", t=PACK))
        w0_plane = zeroed_plane("w0_plane", R, nc.vector)
        xo_plane = zeroed_plane("xo_plane", T, nc.vector)
        w_plane = zeroed_plane("w_plane", R, nc.vector)
        xt_plane = zeroed_plane("xt_plane", T, nc.vector)
        wb_plane = zeroed_plane("wb_plane", N, nc.vector)

        ca_sb = [None] * PACK
        ca_sb[0] = load_ca(0)
        l3 = load_list("l3", offs3)
        l4 = load_list("l4", offs4)
        ca_sb[1] = load_ca(1)
        l2 = load_list("l2", offs2)
        l1 = load_list("l1", offs)
        ca_sb[2] = load_ca(2)
        xo_sb = load_words("xo_sb", xo_words[0], T, U16)
        w0_sb = load_words("w0_sb", w0_words[0].rearrange("p c b -> p (c b)"), R, U32)
        load_scales(w0_plane, w0_scales, nc.sync, range(4))
        load_scales(xo_plane, xo_scales, nc.sync, range(4))
        ca_sb[3] = load_ca(3)
        w_sb = load_words("w_sb", w_words[0], R, U16)
        load_scales(w_plane, w_scales, nc.sync, range(4))
        xt_sb = load_words("xt_sb", xt_words[0].rearrange("p c b -> p (c b)"), T, I32)
        load_scales(xt_plane, xt_scales, nc.sync, range(4))
        wb_sb = load_words("wb_sb", wb_words[0].rearrange("p c b -> p (c b)"), N, I32)
        load_scales(wb_plane, wb_scales, nc.sync, range(4))

        ident = tile("ident", [P, P], F32)
        make_identity(nc, ident[:])

        def look_up(name, lst, t, values, scale):
            got = tile("%s_%d" % (name, t), [P, J], U8)
            nc.vector.tensor_copy(got[:], ca_sb[t][:].indirect(lst[:]))
            nc.scalar.activation(values, got[:].bitcast(FP8), ACT.Copy, scale=scale)

        turned_ps = ps.tile([P, EARLY, HALVES, P], F32, name="turned_ps")
        for t in range(EARLY):
            plus = tile("plus%d" % t, [P, J], F32)
            minus = tile("minus%d" % t, [P, J], F32)
            look_up("g3", l3, t, plus[:], 1.0)
            look_up("g4", l4, t, minus[:], -1.0)
            for h in range(HALVES):
                cols = slice(h * P, (h + 1) * P)
                nc.tensor.matmul(turned_ps[:, t, h, :], plus[:, cols], ident[:], start=True, stop=False, is_transpose=True)
                nc.tensor.matmul(turned_ps[:, t, h, :], minus[:, cols], ident[:], start=False, stop=True, is_transpose=True)
        turned = tile("turned", [P, EARLY, HALVES, P], F32)
        nc.scalar.copy(turned[:], turned_ps[:])
        early_ps = ps.tile([P, HALVES, EARLY, P], F32, name="early_ps")
        for t in range(EARLY):
            for h in range(HALVES):
                nc.tensor.transpose(early_ps[:, h, t, :], turned[:, t, h, :], ident[:])

        s3 = tile("s3", [P, PACK - EARLY, J], F32)
        s4 = tile("s4", [P, PACK - EARLY, J], F32)
        for t in range(EARLY, PACK):
            look_up("g3", l3, t, s3[:, t - EARLY, :], st_sb[:, t : t + 1])
            look_up("g4", l4, t, s4[:, t - EARLY, :], st_sb[:, t : t + 1])

        def dealt(name, words, plane, dtype):
            dealt_words = tile(name + "_words", [P, PACK, P], dtype)
            nc.scalar.copy(dealt_words[:].rearrange("k t (c i) -> k c t i", i=4), words[:].rearrange("k (c i t) -> k c t i", i=4, t=PACK))
            dealt_plane = tile(name + "_plane", [P, PACK, P], U8)
            nc.gpsimd.tensor_copy(dealt_plane[:], plane[:].rearrange("k (m t) -> k t m", t=PACK))
            return dealt_words, dealt_plane

        w0_d, w0_ds = dealt("w0_d", w0_sb, w0_plane, U32)
        w_d, w_ds = dealt("w_d", w_sb, w_plane, U16)

        a_ps = [ps.tile([P, PACK, P], F32, name="a_ps%d" % h) for h in range(HALVES)]
        xo_g = tile("xo_g", [P, J], U16)
        nc.vector.tensor_copy(xo_g[:], xo_sb[:].indirect(l2[:]))
        xo_gs = tile("xo_gs", [P, J], U8)
        nc.vector.tensor_copy(xo_gs[:], xo_plane[:].indirect(l2[:]))
        for h in range(HALVES):
            cols = slice(h * P, (h + 1) * P)
            for t in range(PACK):
                nc.tensor.matmul_mx(a_ps[h][:, t, :], lhsT=w0_d[:, t, :].bitcast(E5M2X4), lhsT_scale=w0_ds[:, t, :],
                                    rhs=xo_g[:, cols].bitcast(E2M1X4), rhs_scale=xo_gs[:, cols], start=t == 0, stop=False)
        xt_g = tile("xt_g", [P, J], U32)
        nc.vector.tensor_copy(xt_g[:], xt_sb[:].bitcast(U32).indirect(l1[:]))
        for h in range(HALVES):
            cols = slice(h * P, (h + 1) * P)
            xt_gs = tile("xt_gs%d" % h, [P, P], U8)
            nc.vector.tensor_copy(xt_gs[:], xt_plane[:].indirect(l1[:, h * P // 16 : (h + 1) * P // 16]))
            for t in range(PACK):
                nc.tensor.matmul_mx(a_ps[h][:, t, :], lhsT=w_d[:, t, :].bitcast(E2M1X4), lhsT_scale=w_ds[:, t, :],
                                    rhs=xt_g[:, cols].bitcast(E4M3X4), rhs_scale=xt_gs[:], start=False, stop=t == PACK - 1)

        d = tile("d", [P, HALVES, PACK, P], F32, tag="xt_plane")
        for h in range(HALVES):
            cols = slice(h * P, (h + 1) * P)
            for t in range(EARLY):
                nc.scalar.activation(d[:, h, t, :], early_ps[:, h, t, :], ACT.Copy, scale=st_sb[:, t : t + 1])
            nc.vector.tensor_tensor(d[:, h, EARLY:PACK, :], s3[:, :, cols], s4[:, :, cols], ALU.subtract)

        hid = [tile("hid%d" % h, [P, P * PACK], BF16) for h in range(HALVES)]
        for h in range(HALVES):
            nc.vector.tensor_tensor(
                hid[h][:].rearrange("p (c i t) -> p c t i", i=2, t=PACK),
                a_ps[h][:].rearrange("p t (c i) -> p c t i", i=2),
                d[:, h].rearrange("p t (c i) -> p c t i", i=2),
                ALU.mult,
            )
        hq = [tile("hq%d" % h, [P, P], U32) for h in range(HALVES)]
        hq_plane = [tile("hq_plane%d" % h, [P, P], U8) for h in range(HALVES)]
        for h in range(HALVES):
            nc.vector.quantize_mx(hq[h][:].bitcast(E4M3X4), hq_plane[h][:], hid[h][:])

        for h in range(HALVES):
            cols = slice(h * P, (h + 1) * P)
            for m in range(N // P):
                rows = slice(m * P, (m + 1) * P)
                o_ps = ps.tile([P, P], F32, name="o_ps%d_%d" % (h, m))
                nc.tensor.matmul_mx(o_ps[:], lhsT=wb_sb[:, rows].bitcast(E5M2X4), lhsT_scale=wb_plane[:, rows],
                                    rhs=hq[h][:].bitcast(E4M3X4), rhs_scale=hq_plane[h][:], start=True, stop=True)
                o_sb = tile("o_sb%d_%d" % (h, m), [P, P], F32)
                if m == 0:
                    nc.scalar.copy(o_sb[:], o_ps[:])
                else:
                    nc.vector.tensor_copy(o_sb[:], o_ps[:])
                queue = nc.scalar if (h, m) == (1, 0) else nc.sync
                queue.dma_start(out[rows, cols], o_sb[:])
